import numpy as np
import ml_dtypes


def mxq(x, axis, fmt="e4m3"):
    dtype, down = {"e4m3": (ml_dtypes.float8_e4m3fn, 7), "e5m2": (ml_dtypes.float8_e5m2, 14)}[fmt]
    v = np.moveaxis(np.asarray(x, np.float32).astype(ml_dtypes.bfloat16).astype(np.float64), axis, -1)
    blocks = v.reshape(v.shape[:-1] + (-1, 32))
    amax = np.abs(blocks).max(-1, keepdims=True)
    byte = np.maximum(np.where(amax > 0, np.frexp(amax)[1] - 1 + 127, 0) - down, 1)
    scale = np.exp2(byte - 127.0)
    codes = (blocks / scale).astype(np.float32).astype(dtype).astype(np.float64)
    return np.moveaxis((codes * scale).reshape(v.shape), -1, axis)


WIDE = False


def mx_kscale(k):
    if not WIDE:
        return np.ones(k)
    levels = np.array([10, -10, 5, -5, 0])
    if k % 512:
        return np.exp2(np.random.permutation(np.resize(levels, k // 32))).repeat(32)
    a = np.empty((k // 512, 16))
    for p in range(k // 512):
        a[p, :8] = np.random.permutation(np.resize(levels, 8))
        for g in range(8):
            far = levels[np.abs(levels - a[p, g]) >= 10]
            a[p, g + 8] = far[np.random.randint(len(far))]
    return np.exp2(a.ravel()).repeat(32)


BF16 = ml_dtypes.bfloat16


def bf(x):
    return np.asarray(x, np.float32).astype(BF16)


def f64(x):
    return np.asarray(x).astype(np.float64)


B, H, W, G, P, R, K = 4, 32, 32, 128, 8, 512, 3
C = G * P
TAPS = K * K
O = TAPS * G


def sigmoid(v):
    return 1.0 / (1.0 + np.exp(-v))


def draw0():
    s, t = mx_kscale(C), mx_kscale(R)
    return {
        "x": bf(np.random.standard_normal((B, H, W, C)) * s),
        "w1": bf(np.random.standard_normal((C, R)) / np.sqrt(C) / s[:, None]),
        "b1": bf(0.3 * np.random.standard_normal(R)),
        "g1": bf((1.0 + 0.1 * np.random.standard_normal(R)) * t),
        "w2": bf(np.random.standard_normal((R, O)) / np.sqrt(R) / t[:, None]),
        "gv": bf((1.0 + 0.1 * np.random.standard_normal(C)) / s),
    }


def make_kernels(x, w1, b1, g1, w2):
    h = (mxq(x, 3, "e4m3") @ mxq(w1, 0, "e4m3")) + b1
    z = h * sigmoid(h) * g1
    k = mxq(z, 3, "e4m3") @ mxq(w2, 0, "e4m3")
    nb, nh, nw, _ = k.shape
    return k.reshape(nb, nh, nw, TAPS, G)


def tap_term(k, xp, di, dj):
    nh = k.shape[1]
    nw = k.shape[2]
    window = xp[:, di:di + nh, dj:dj + nw, :, :]
    weight = k[:, :, :, K * di + dj, :]
    return weight[..., None] * window


def core(x, w1, b1, g1, w2, gv):
    x = f64(x)
    nb, nh, nw, nc = x.shape
    k = make_kernels(x, f64(w1), f64(b1), f64(g1), f64(w2))

    xv = x * f64(gv)
    pad = K // 2
    xp = np.pad(xv, ((0, 0), (pad, pad), (pad, pad), (0, 0)))
    xp = xp.reshape(nb, xp.shape[1], xp.shape[2], G, P)

    y = np.zeros((nb, nh, nw, G, P))
    for di in range(K):
        for dj in range(K):
            y = y + tap_term(k, xp, di, dj)
    return y.reshape(nb, nh, nw, nc)


def e4m3fn_bytes(y):
    return np.clip(np.asarray(y, np.float64), -448.0, 448.0).astype(np.float32).astype(ml_dtypes.float8_e4m3fn).view(np.uint8)


def e4m3fn_values(b):
    return np.asarray(b, np.uint8).view(ml_dtypes.float8_e4m3fn).astype(np.float64)


def setup_inputs():
    d = draw0()
    x0 = np.asarray(d['w2']).astype(np.float64)
    s = (np.max(np.abs(x0), axis=(1,), keepdims=True) / 448.0).astype(np.float32)
    out = {}
    for k, v in d.items():
        if k == 'w2':
            out['w2_bytes'] = e4m3fn_bytes(x0 / s.astype(np.float64))
            out['w2_scale'] = s
        else:
            out[k] = v
    return out


def reference(x, w1, b1, g1, w2_bytes, w2_scale, gv):
    return core(x, w1, b1, g1, e4m3fn_values(w2_bytes) * w2_scale.astype(np.float64), gv)

@@ -1,0 +1,306 @@
+from contextlib import ExitStack
+
+import concourse.mybir as mybir
+from concourse.masks import make_identity
+
+B, H, W, C, R, G, J = 4, 32, 32, 1024, 512, 128, 8
+O = 9 * G
+FLOPS = 2 * B * H * W * (C * R + R * O) + 2 * 9 * B * H * W * C
+
+F32 = mybir.dt.float32
+BF16 = mybir.dt.bfloat16
+U32 = mybir.dt.uint32
+U8 = mybir.dt.uint8
+FP8 = mybir.dt.float8_e4m3fn
+FP8X4 = mybir.dt.float8_e4m3fn_x4
+ACT = mybir.ActivationFunctionType
+MULT = mybir.AluOpType.mult
+
+P = 128
+SEG = P + B
+XV_ROW = J * SEG + SEG
+XV_SLOTS = 5
+BANK_TAPS = ([(0, 0), (0, 2), (1, 0)], [(1, 2), (2, 0), (2, 2)])
+SPARE = 3
+LOAD_AHEAD = 9
+FIRST_STEP = -7
+
+
+def tile_bottleneckinvolutionthreebythree_t_kernel(tc, x, w1, b1, g1, w2_bytes, w2_scale, gv, out):
+    nc = tc.nc
+
+    def inside(row):
+        return 0 <= row < H
+
+    with ExitStack() as ctx:
+        keep = ctx.enter_context(tc.tile_pool(name="keep", bufs=1))
+        work = ctx.enter_context(tc.tile_pool(name="work", bufs=2))
+        prods = ctx.enter_context(tc.tile_pool(name="prods", bufs=3))
+        psum = ctx.enter_context(tc.psum_pool(name="psum", bufs=2))
+        ctx.enter_context(tc.manual_schedule())
+
+        x_pairs, mx_words, inv_words, x_grouped, x_quant = {}, {}, {}, {}, {}
+        z_grouped, z_quant, k_banks, k_mid, prod_v, prod_g, out_rows = {}, {}, {}, {}, {}, {}, {}
+
+        def load_pair(row):
+            pair = work.tile([P, 2, C], BF16, name="x_pair", bufs=4)
+            for b in range(B):
+                nc.sync.dma_start(out=pair[b:P:B, :, :], in_=x[b, row:row + 2].rearrange("i w c -> w i c"))
+            x_pairs[row] = pair
+
+        load_pair(0)
+        w1_raw = prods.tile([P, 2, 4, R], BF16, name="w1_raw", tag="pg", align_bytes=64)
+        for half in range(2):
+            nc.sync.dma_start(out=w1_raw[:, half],
+                              in_=w1[512 * half:512 * (half + 1), :].rearrange("(p j) r -> p j r", j=4))
+        w2_rows = w2_bytes.rearrange("(p t) n -> p t n", t=4)
+        w2_raw = []
+        for half in range(2):
+            raw_bytes = keep.tile([P, 2, O], U8, name="w2_raw%d" % half)
+            nc.sync.dma_start(out=raw_bytes[:], in_=w2_rows[:, 2 * half:2 * half + 2, :])
+            w2_raw.append(raw_bytes)
+        w2_sc = keep.tile([P, 4], F32, name="w2_sc")
+        nc.sync.dma_start(out=w2_sc[:], in_=w2_scale.rearrange("(p t) o -> p (t o)", t=4))
+        b1_raw = keep.tile([P, 4], BF16, name="b1_raw")
+        nc.sync.dma_start(out=b1_raw[:], in_=b1.rearrange("(p t) -> p t", t=4))
+        g1_raw = keep.tile([P, 4], BF16, name="g1_raw")
+        nc.sync.dma_start(out=g1_raw[:], in_=g1.rearrange("(p t) -> p t", t=4))
+        gv_raw = keep.tile([P, J], BF16, name="gv_raw")
+        nc.sync.dma_start(out=gv_raw[:], in_=gv.rearrange("(p j) -> p j", j=J))
+
+        ident = keep.tile([P, P], F32, name="ident")
+        make_identity(nc, ident[:])
+        xv = keep.tile([P, XV_SLOTS, XV_ROW], F32, name="xv")
+        for slot in range(XV_SLOTS):
+            nc.gpsimd.memset(xv[:, slot].rearrange("p (j c) -> p j c", c=SEG)[:, :, 0:B], 0.0)
+
+        w1_grouped = prods.tile([P, 2, R, 4], BF16, name="w1_grouped", tag="pg", align_bytes=64)
+        for half in range(2):
+            nc.vector.tensor_copy(out=w1_grouped[:, half].rearrange("p (t m) j -> p t m j", t=4),
+                                  in_=w1_raw[:, half].rearrange("p j (m t) -> p t m j", t=4))
+        w1_codes = keep.tile([P, 2, R], U32, name="w1_codes", align_bytes=64)
+        w1_scales = keep.tile([P, 2, R], U8, name="w1_scales", align_bytes=64)
+        nc.vector.quantize_mx(out=w1_codes[:].rearrange("p g r -> p (g r)").bitcast(FP8X4),
+                              scales=w1_scales[:].rearrange("p g r -> p (g r)"),
+                              in_=w1_grouped[:].rearrange("p g r j -> p (g r j)"))
+        b1_col = keep.tile([P, 4], F32, name="b1_col")
+        g1_col = keep.tile([P, 4], F32, name="g1_col")
+        gv_col = keep.tile([P, J], F32, name="gv_col")
+        nc.vector.tensor_copy(out=b1_col[:], in_=b1_raw[:])
+        nc.vector.tensor_copy(out=g1_col[:], in_=g1_raw[:])
+        nc.vector.tensor_copy(out=gv_col[:], in_=gv_raw[:])
+
+        w2_codes = keep.tile([P, O], U32, name="w2_codes", align_bytes=64)
+        w2_scales = keep.tile([P, O], U8, name="w2_scales", align_bytes=64)
+
+        def prepare_w2():
+            planes = prods.tile([P, 4, O], BF16, name="w2_planes", tag="pg", align_bytes=64)
+            for t in range(4):
+                nc.vector.tensor_scalar(out=planes[:, t, :], in0=w2_raw[t // 2][:, t % 2, :].bitcast(FP8),
+                                        scalar1=w2_sc[:, t:t + 1], scalar2=None, op0=MULT)
+            grouped = prods.tile([P, O, 4], BF16, name="w2_grouped", tag="pv", align_bytes=64)
+            nc.vector.tensor_copy(out=grouped[:].rearrange("p (c i) t -> p c t i", i=4),
+                                  in_=planes[:].rearrange("p t (c i) -> p c t i", i=4))
+            for lo, hi in ((0, 1024), (1024, O)):
+                nc.vector.quantize_mx(out=w2_codes[:, lo:hi].bitcast(FP8X4), scales=w2_scales[:, lo:hi],
+                                      in_=grouped[:, lo:hi, :].rearrange("p c t -> p (c t)"))
+
+        def row_words(row):
+            return x_pairs[row - row % 2][:, row % 2, :].bitcast(F32)
+
+        def arrange_mx(row):
+            words = work.tile([P, 512], F32, name="mx_words")
+            nc.scalar.copy(out=words[:].rearrange("p (g u q i) -> p g q u i", g=2, u=2, i=4),
+                           in_=row_words(row).rearrange("p (g q i u) -> p g q u i", g=2, i=4, u=2))
+            mx_words[row] = words
+
+        def arrange_inv(row):
+            words = work.tile([P, 512], F32, name="inv_words")
+            nc.scalar.copy(out=words[:].rearrange("p (u q i) -> p q u i", u=4, i=4),
+                           in_=row_words(row).rearrange("p (q i u) -> p q u i", i=4, u=4))
+            inv_words[row] = words
+
+        def turn(words):
+            bank = psum.tile([P, 4, P], F32, name="misc")
+            for n in range(4):
+                nc.tensor.transpose(bank[:, n, :], words[:, P * n:P * (n + 1)], ident[:])
+            return bank
+
+        def empty_mx(row, bank):
+            if row % 2 == 0:
+                x_grouped[row] = work.tile([P, 2, 2, P * 4], BF16, name="x_grouped", align_bytes=64)
+            grouped = x_grouped[row - row % 2]
+            nc.scalar.copy(out=grouped[:, :, row % 2, :].bitcast(F32).rearrange("p g (q u) -> p g q u", u=2),
+                           in_=bank[:].rearrange("p (g u) q -> p g q u", u=2))
+
+        def empty_inv(row, bank):
+            halves = bank[:].bitcast(BF16).rearrange("p u (q e) -> p u q e", e=2)
+            for j in range(J):
+                lo = j * SEG + B
+                nc.scalar.activation(out=xv[:, row % XV_SLOTS, lo:lo + P], in_=halves[:, j // 2, :, j % 2],
+                                     func=ACT.Copy, scale=gv_col[:, j:j + 1])
+
+        def quantize_x(row):
+            codes = work.tile([P, 2, 2, P], U32, name="x_codes", align_bytes=64)
+            scales = work.tile([P, 2, 2, P], U8, name="x_scales", align_bytes=64)
+            nc.vector.quantize_mx(out=codes[:].rearrange("p g h q -> p (g h q)").bitcast(FP8X4),
+                                  scales=scales[:].rearrange("p g h q -> p (g h q)"),
+                                  in_=x_grouped[row][:].rearrange("p g h c -> p (g h c)"))
+            x_quant[row] = (codes, scales)
+
+        def quantize_z(row):
+            codes = work.tile([P, 2, P], U32, name="z_codes", align_bytes=64)
+            scales = work.tile([P, 2, P], U8, name="z_scales", align_bytes=64)
+            nc.vector.quantize_mx(out=codes[:].rearrange("p h q -> p (h q)").bitcast(FP8X4),
+                                  scales=scales[:].rearrange("p h q -> p (h q)"),
+                                  in_=z_grouped[row][:].rearrange("p h q t -> p (h q t)"))
+            z_quant[row] = (codes, scales)
+
+        def hidden_matmuls(row):
+            codes, scales = x_quant[row - row % 2]
+            bank = psum.tile([P, 4, P], F32, name="misc")
+            for t in range(4):
+                cols = slice(P * t, P * (t + 1))
+                for half in range(2):
+                    nc.tensor.matmul_mx(out=bank[:, t, :],
+                                        lhsT=w1_codes[:, half, cols].bitcast(FP8X4), lhsT_scale=w1_scales[:, half, cols],
+                                        rhs=codes[:, half, row % 2, :].bitcast(FP8X4), rhs_scale=scales[:, half, row % 2, :],
+                                        start=(half == 0), stop=(half == 1))
+            return bank
+
+        def activate(row, bank):
+            gated = work.tile([P, 4, P], F32, name="gated")
+            for t in range(4):
+                nc.scalar.activation(out=gated[:, t, :], in_=bank[:, t, :], func=ACT.Silu, bias=b1_col[:, t:t + 1])
+            planes = work.tile([P, 4, P], BF16, name="z_planes")
+            for t in range(4):
+                nc.scalar.activation(out=planes[:, t, :], in_=gated[:, t, :], func=ACT.Copy, scale=g1_col[:, t:t + 1])
+            if row % 2 == 0:
+                z_grouped[row] = work.tile([P, 2, P, 4], BF16, name="z_grouped", align_bytes=64)
+            nc.scalar.copy(out=z_grouped[row - row % 2][:, row % 2].rearrange("p (c i) t -> p c t i", i=4),
+                           in_=planes[:].rearrange("p t (c i) -> p c t i", i=4))
+
+        def tap_matmul(row, tap, dest):
+            codes, scales = z_quant[row - row % 2]
+            n = 3 * tap[0] + tap[1]
+            cols = slice(G * n, G * (n + 1))
+            nc.tensor.matmul_mx(out=dest, lhsT=w2_codes[:, cols].bitcast(FP8X4), lhsT_scale=w2_scales[:, cols],
+                                rhs=codes[:, row % 2, :].bitcast(FP8X4), rhs_scale=scales[:, row % 2, :],
+                                start=True, stop=True)
+
+        def mid_rows(row):
+            return [di for di in range(3) if inside(row + di - 1)]
+
+        def kernel_matmuls(row):
+            mid_bank = psum.tile([P, 4, P], F32, name="misc")
+            by_scalar = [di for di in mid_rows(row) if not (row % 2 == 1 and di == 1)]
+            for di in by_scalar:
+                tap_matmul(row, (di, 1), mid_bank[:, di, :])
+            banks = []
+            for n, taps in enumerate(BANK_TAPS):
+                bank = psum.tile([P, 4, P], F32, name="k_bank%d" % n)
+                for s, tap in enumerate(taps):
+                    if inside(row + tap[0] - 1):
+                        tap_matmul(row, tap, bank[:, s, :])
+                if n == 0 and row % 2 == 1:
+                    tap_matmul(row, (1, 1), bank[:, SPARE, :])
+                banks.append(bank)
+            k_banks[row] = banks
+            return mid_bank, by_scalar
+
+        def empty_mid(row, mid_bank, by_scalar):
+            mid = work.tile([P, 3, P], F32, name="k_mid", bufs=3)
+            step = 2 if by_scalar == [0, 2] else 1
+            sel = slice(by_scalar[0], by_scalar[-1] + 1, step)
+            nc.scalar.copy(out=mid[:, sel, :], in_=mid_bank[:, sel, :])
+            k_mid[row] = mid
+
+        def shifted(row, dj):
+            lo = B * dj
+            return xv[:, row % XV_SLOTS, lo:lo + J * SEG].rearrange("p (j c) -> p j c", c=SEG)[:, :, 0:P]
+
+        def side_products(row):
+            prod = prods.tile([P, 6, J, P], F32, name="prod_v", tag="pv", align_bytes=64)
+            for n, taps in enumerate(BANK_TAPS):
+                for s, (di, dj) in enumerate(taps):
+                    if inside(row + di - 1):
+                        nc.vector.tensor_tensor(out=prod[:, 3 * n + s],
+                                                in0=k_banks[row][n][:, s, :].unsqueeze(1).to_broadcast([P, J, P]),
+                                                in1=shifted(row + di - 1, dj), op=MULT)
+            prod_v[row] = prod
+
+        def mid_products(row):
+            prod = prods.tile([P, 3, J, P], F32, name="prod_g", tag="pg", align_bytes=64)
+            runs = []
+            for di in mid_rows(row):
+                if runs and (row + di - 1) % XV_SLOTS != 0:
+                    runs[-1].append(di)
+                else:
+                    runs.append([di])
+            for run in runs:
+                lo, n = run[0], len(run)
+                slot = (row + lo - 1) % XV_SLOTS
+                window = xv[:, slot:slot + n, B:B + J * SEG].rearrange("p d (j c) -> p d j c", c=SEG)[:, :, :, 0:P]
+                nc.gpsimd.tensor_tensor(out=prod[:, lo:lo + n],
+                                        in0=k_mid[row][:, lo:lo + n, :].unsqueeze(2).to_broadcast([P, n, J, P]),
+                                        in1=window, op=MULT)
+            prod_g[row] = prod
+
+        def sum_taps(row, half):
+            terms = [prod_v[row][:, 3 * n + s] for n, taps in enumerate(BANK_TAPS)
+                     for s, tap in enumerate(taps) if inside(row + tap[0] - 1)]
+            terms = terms + [prod_g[row][:, di] for di in mid_rows(row)]
+            bank = psum.tile([P, 4, P], F32, name="out_bank")
+            for jj in range(4):
+                for n, term in enumerate(terms):
+                    nc.tensor.matmul(bank[:, jj, :], lhsT=term[:, 4 * half + jj, :], rhs=ident[:], is_transpose=True,
+                                     start=(n == 0), stop=(n == len(terms) - 1))
+            if half == 0:
+                out_rows[row] = work.tile([P, G, J], F32, name="out_row", bufs=3)
+            nc.scalar.copy(out=out_rows[row][:, :, 4 * half:4 * half + 4], in_=bank[:].rearrange("p j g -> p g j"))
+
+        def store_row(row):
+            flat = out_rows[row][:].rearrange("p g j -> p (g j)")
+            for b in range(B):
+                nc.sync.dma_start(out=out[b, row], in_=flat[b:P:B, :])
+
+        for m in range(FIRST_STEP, H):
+            if m % 2 == 1 and inside(m + LOAD_AHEAD):
+                load_pair(m + LOAD_AHEAD)
+            if m % 2 == 0:
+                if inside(m + 4):
+                    quantize_x(m + 4)
+                if m == -4:
+                    prepare_w2()
+                if inside(m + 2):
+                    quantize_z(m + 2)
+                if inside(m + 1):
+                    nc.vector.tensor_copy(out=k_mid[m + 1][:, 1, :], in_=k_banks[m + 1][0][:, SPARE, :])
+            if inside(m + 1):
+                mid_products(m + 1)
+                side_products(m + 1)
+            if inside(m + 6):
+                mx_bank = turn(mx_words[m + 6])
+            if inside(m + 3):
+                inv_bank = turn(inv_words[m + 3])
+            if inside(m + 6):
+                empty_mx(m + 6, mx_bank)
+            if inside(m + 3):
+                empty_inv(m + 3, inv_bank)
+            if inside(m + 7):
+                arrange_mx(m + 7)
+            if inside(m + 4):
+                arrange_inv(m + 4)
+            if inside(m):
+                sum_taps(m, 0)
+            if inside(m + 2):
+                mid_bank, by_scalar = kernel_matmuls(m + 2)
+            if inside(m + 4):
+                hidden_bank = hidden_matmuls(m + 4)
+            if inside(m + 2):
+                empty_mid(m + 2, mid_bank, by_scalar)
+            if inside(m + 4):
+                activate(m + 4, hidden_bank)
+            if inside(m):
+                sum_taps(m, 1)
+                store_row(m)

@@ -193,7 +193,7 @@ def tile_bottleneckinvolutionthreebythree_t_kernel(tc, x, w1, b1, g1, w2_bytes, 
 
         def kernel_matmuls(row):
             mid_bank = psum.tile([P, 4, P], F32, name="misc")
-            by_scalar = [di for di in mid_rows(row) if not (row % 2 == 1 and di == 1)]
+            by_scalar = [di for di in mid_rows(row) if di != (1 if row % 2 == 1 else 2)]
             for di in by_scalar:
                 tap_matmul(row, (di, 1), mid_bank[:, di, :])
             banks = []
@@ -204,6 +204,8 @@ def tile_bottleneckinvolutionthreebythree_t_kernel(tc, x, w1, b1, g1, w2_bytes, 
                         tap_matmul(row, tap, bank[:, s, :])
                 if n == 0 and row % 2 == 1:
                     tap_matmul(row, (1, 1), bank[:, SPARE, :])
+                if n == 1 and row % 2 == 0:
+                    tap_matmul(row, (2, 1), bank[:, SPARE, :])
                 banks.append(bank)
             k_banks[row] = banks
             return mid_bank, by_scalar
@@ -227,12 +229,18 @@ def tile_bottleneckinvolutionthreebythree_t_kernel(tc, x, w1, b1, g1, w2_bytes, 
                         nc.vector.tensor_tensor(out=prod[:, 3 * n + s],
                                                 in0=k_banks[row][n][:, s, :].unsqueeze(1).to_broadcast([P, J, P]),
                                                 in1=shifted(row + di - 1, dj), op=MULT)
+            if row % 2 == 0:
+                nc.vector.tensor_tensor(out=prod_g[row][:, 2],
+                                        in0=k_banks[row][1][:, SPARE, :].unsqueeze(1).to_broadcast([P, J, P]),
+                                        in1=shifted(row + 1, 1), op=MULT)
             prod_v[row] = prod
 
         def mid_products(row):
             prod = prods.tile([P, 3, J, P], F32, name="prod_g", tag="pg", align_bytes=64)
             runs = []
             for di in mid_rows(row):
+                if row % 2 == 0 and di == 2:
+                    continue
                 if runs and (row + di - 1) % XV_SLOTS != 0:
                     runs[-1].append(di)
                 else:
@@ -293,14 +301,14 @@ def tile_bottleneckinvolutionthreebythree_t_kernel(tc, x, w1, b1, g1, w2_bytes, 
                 arrange_inv(m + 4)
             if inside(m):
                 sum_taps(m, 0)
-            if inside(m + 2):
-                mid_bank, by_scalar = kernel_matmuls(m + 2)
             if inside(m + 4):
                 hidden_bank = hidden_matmuls(m + 4)
             if inside(m + 2):
-                empty_mid(m + 2, mid_bank, by_scalar)
+                mid_bank, by_scalar = kernel_matmuls(m + 2)
             if inside(m + 4):
                 activate(m + 4, hidden_bank)
+            if inside(m + 2):
+                empty_mid(m + 2, mid_bank, by_scalar)
             if inside(m):
                 sum_taps(m, 1)
                 store_row(m)

@@ -15,6 +15,7 @@ FP8 = mybir.dt.float8_e4m3fn
 FP8X4 = mybir.dt.float8_e4m3fn_x4
 ACT = mybir.ActivationFunctionType
 MULT = mybir.AluOpType.mult
+ADD = mybir.AluOpType.add
 
 P = 128
 SEG = P + B
@@ -191,11 +192,14 @@ def tile_bottleneckinvolutionthreebythree_t_kernel(tc, x, w1, b1, g1, w2_bytes, 
         def mid_rows(row):
             return [di for di in range(3) if inside(row + di - 1)]
 
-        def kernel_matmuls(row):
+        def mid_matmuls(row):
             mid_bank = psum.tile([P, 4, P], F32, name="misc")
-            by_scalar = [di for di in mid_rows(row) if di != (1 if row % 2 == 1 else 2)]
+            by_scalar = [di for di in mid_rows(row) if di == 0 or (di == 1 and row % 2 == 0)]
             for di in by_scalar:
                 tap_matmul(row, (di, 1), mid_bank[:, di, :])
+            return mid_bank, by_scalar
+
+        def side_matmuls(row):
             banks = []
             for n, taps in enumerate(BANK_TAPS):
                 bank = psum.tile([P, 4, P], F32, name="k_bank%d" % n)
@@ -204,16 +208,14 @@ def tile_bottleneckinvolutionthreebythree_t_kernel(tc, x, w1, b1, g1, w2_bytes, 
                         tap_matmul(row, tap, bank[:, s, :])
                 if n == 0 and row % 2 == 1:
                     tap_matmul(row, (1, 1), bank[:, SPARE, :])
-                if n == 1 and row % 2 == 0:
+                if n == 1 and inside(row + 1):
                     tap_matmul(row, (2, 1), bank[:, SPARE, :])
                 banks.append(bank)
             k_banks[row] = banks
-            return mid_bank, by_scalar
 
         def empty_mid(row, mid_bank, by_scalar):
-            mid = work.tile([P, 3, P], F32, name="k_mid", bufs=3)
-            step = 2 if by_scalar == [0, 2] else 1
-            sel = slice(by_scalar[0], by_scalar[-1] + 1, step)
+            mid = work.tile([P, 2, P], F32, name="k_mid", bufs=3)
+            sel = slice(by_scalar[0], by_scalar[-1] + 1)
             nc.scalar.copy(out=mid[:, sel, :], in_=mid_bank[:, sel, :])
             k_mid[row] = mid
 
@@ -229,7 +231,7 @@ def tile_bottleneckinvolutionthreebythree_t_kernel(tc, x, w1, b1, g1, w2_bytes, 
                         nc.vector.tensor_tensor(out=prod[:, 3 * n + s],
                                                 in0=k_banks[row][n][:, s, :].unsqueeze(1).to_broadcast([P, J, P]),
                                                 in1=shifted(row + di - 1, dj), op=MULT)
-            if row % 2 == 0:
+            if inside(row + 1):
                 nc.vector.tensor_tensor(out=prod_g[row][:, 2],
                                         in0=k_banks[row][1][:, SPARE, :].unsqueeze(1).to_broadcast([P, J, P]),
                                         in1=shifted(row + 1, 1), op=MULT)
@@ -239,7 +241,7 @@ def tile_bottleneckinvolutionthreebythree_t_kernel(tc, x, w1, b1, g1, w2_bytes, 
             prod = prods.tile([P, 3, J, P], F32, name="prod_g", tag="pg", align_bytes=64)
             runs = []
             for di in mid_rows(row):
-                if row % 2 == 0 and di == 2:
+                if di == 2:
                     continue
                 if runs and (row + di - 1) % XV_SLOTS != 0:
                     runs[-1].append(di)
@@ -254,10 +256,17 @@ def tile_bottleneckinvolutionthreebythree_t_kernel(tc, x, w1, b1, g1, w2_bytes, 
                                         in1=window, op=MULT)
             prod_g[row] = prod
 
+        def side_terms(row):
+            return [prod_v[row][:, 3 * n + s] for n, taps in enumerate(BANK_TAPS)
+                    for s, tap in enumerate(taps) if inside(row + tap[0] - 1)]
+
+        def add_first_pair(row):
+            first, second = side_terms(row)[0:2]
+            nc.gpsimd.tensor_tensor(out=first, in0=first, in1=second, op=ADD)
+
         def sum_taps(row, half):
-            terms = [prod_v[row][:, 3 * n + s] for n, taps in enumerate(BANK_TAPS)
-                     for s, tap in enumerate(taps) if inside(row + tap[0] - 1)]
-            terms = terms + [prod_g[row][:, di] for di in mid_rows(row)]
+            sides = side_terms(row)
+            terms = sides[2:] + [prod_g[row][:, di] for di in mid_rows(row)] + sides[0:1]
             bank = psum.tile([P, 4, P], F32, name="out_bank")
             for jj in range(4):
                 for n, term in enumerate(terms):
@@ -287,6 +296,7 @@ def tile_bottleneckinvolutionthreebythree_t_kernel(tc, x, w1, b1, g1, w2_bytes, 
             if inside(m + 1):
                 mid_products(m + 1)
                 side_products(m + 1)
+                add_first_pair(m + 1)
             if inside(m + 6):
                 mx_bank = turn(mx_words[m + 6])
             if inside(m + 3):
@@ -304,11 +314,14 @@ def tile_bottleneckinvolutionthreebythree_t_kernel(tc, x, w1, b1, g1, w2_bytes, 
             if inside(m + 4):
                 hidden_bank = hidden_matmuls(m + 4)
             if inside(m + 2):
-                mid_bank, by_scalar = kernel_matmuls(m + 2)
+                mid_bank, by_scalar = mid_matmuls(m + 2)
             if inside(m + 4):
                 activate(m + 4, hidden_bank)
             if inside(m + 2):
                 empty_mid(m + 2, mid_bank, by_scalar)
             if inside(m):
                 sum_taps(m, 1)
+            if inside(m + 2):
+                side_matmuls(m + 2)
+            if inside(m):
                 store_row(m)

@@ -33,6 +33,9 @@ def tile_bottleneckinvolutionthreebythree_t_kernel(tc, x, w1, b1, g1, w2_bytes, 
     def inside(row):
         return 0 <= row < H
 
+    def interior(row):
+        return 0 < row < H - 1
+
     with ExitStack() as ctx:
         keep = ctx.enter_context(tc.tile_pool(name="keep", bufs=1))
         work = ctx.enter_context(tc.tile_pool(name="work", bufs=2))
@@ -71,6 +74,8 @@ def tile_bottleneckinvolutionthreebythree_t_kernel(tc, x, w1, b1, g1, w2_bytes, 
 
         ident = keep.tile([P, P], F32, name="ident")
         make_identity(nc, ident[:])
+        zeros = keep.tile([P, P], BF16, name="zeros")
+        nc.gpsimd.memset(zeros[:], 0.0)
         xv = keep.tile([P, XV_SLOTS, XV_ROW], F32, name="xv")
         for slot in range(XV_SLOTS):
             nc.gpsimd.memset(xv[:, slot].rearrange("p (j c) -> p j c", c=SEG)[:, :, 0:B], 0.0)
@@ -173,12 +178,17 @@ def tile_bottleneckinvolutionthreebythree_t_kernel(tc, x, w1, b1, g1, w2_bytes, 
             gated = work.tile([P, 4, P], F32, name="gated")
             for t in range(4):
                 nc.scalar.activation(out=gated[:, t, :], in_=bank[:, t, :], func=ACT.Silu, bias=b1_col[:, t:t + 1])
+            if row % 2 == 0:
+                z_grouped[row] = work.tile([P, 2, P, 4], BF16, name="z_grouped", align_bytes=64)
+            grouped = z_grouped[row - row % 2][:, row % 2]
+            if row < 4:
+                nc.vector.tensor_tensor(out=grouped, in0=gated[:].rearrange("p t q -> p q t"),
+                                        in1=g1_col[:].unsqueeze(1).to_broadcast([P, P, 4]), op=MULT)
+                return
             planes = work.tile([P, 4, P], BF16, name="z_planes")
             for t in range(4):
                 nc.scalar.activation(out=planes[:, t, :], in_=gated[:, t, :], func=ACT.Copy, scale=g1_col[:, t:t + 1])
-            if row % 2 == 0:
-                z_grouped[row] = work.tile([P, 2, P, 4], BF16, name="z_grouped", align_bytes=64)
-            nc.scalar.copy(out=z_grouped[row - row % 2][:, row % 2].rearrange("p (c i) t -> p c t i", i=4),
+            nc.scalar.copy(out=grouped.rearrange("p (c i) t -> p c t i", i=4),
                            in_=planes[:].rearrange("p t (c i) -> p c t i", i=4))
 
         def tap_matmul(row, tap, dest):
@@ -266,12 +276,16 @@ def tile_bottleneckinvolutionthreebythree_t_kernel(tc, x, w1, b1, g1, w2_bytes, 
 
         def sum_taps(row, half):
             sides = side_terms(row)
-            terms = sides[2:] + [prod_g[row][:, di] for di in mid_rows(row)] + sides[0:1]
+            mids = [prod_g[row][:, di] for di in mid_rows(row)]
+            terms = sides[2:] + mids + sides[0:1] if interior(row) else sides + mids
             bank = psum.tile([P, 4, P], F32, name="out_bank")
             for jj in range(4):
+                opened = jj > 0
+                if opened:
+                    nc.tensor.matmul(bank[:, jj, :], lhsT=zeros[:], rhs=zeros[:], start=True, stop=False)
                 for n, term in enumerate(terms):
                     nc.tensor.matmul(bank[:, jj, :], lhsT=term[:, 4 * half + jj, :], rhs=ident[:], is_transpose=True,
-                                     start=(n == 0), stop=(n == len(terms) - 1))
+                                     start=(n == 0 and not opened), stop=(n == len(terms) - 1))
             if half == 0:
                 out_rows[row] = work.tile([P, G, J], F32, name="out_row", bufs=3)
             nc.scalar.copy(out=out_rows[row][:, :, 4 * half:4 * half + 4], in_=bank[:].rearrange("p j g -> p g j"))
@@ -296,7 +310,8 @@ def tile_bottleneckinvolutionthreebythree_t_kernel(tc, x, w1, b1, g1, w2_bytes, 
             if inside(m + 1):
                 mid_products(m + 1)
                 side_products(m + 1)
-                add_first_pair(m + 1)
+                if interior(m + 1):
+                    add_first_pair(m + 1)
             if inside(m + 6):
                 mx_bank = turn(mx_words[m + 6])
             if inside(m + 3):
@@ -315,13 +330,11 @@ def tile_bottleneckinvolutionthreebythree_t_kernel(tc, x, w1, b1, g1, w2_bytes, 
                 hidden_bank = hidden_matmuls(m + 4)
             if inside(m + 2):
                 mid_bank, by_scalar = mid_matmuls(m + 2)
+                side_matmuls(m + 2)
             if inside(m + 4):
                 activate(m + 4, hidden_bank)
             if inside(m + 2):
                 empty_mid(m + 2, mid_bank, by_scalar)
             if inside(m):
                 sum_taps(m, 1)
-            if inside(m + 2):
-                side_matmuls(m + 2)
-            if inside(m):
                 store_row(m)

from contextlib import ExitStack

import concourse.mybir as mybir
from concourse.masks import make_identity

B, H, W, C, R, G, J = 4, 32, 32, 1024, 512, 128, 8
O = 9 * G
FLOPS = 2 * B * H * W * (C * R + R * O) + 2 * 9 * B * H * W * C

F32 = mybir.dt.float32
BF16 = mybir.dt.bfloat16
U32 = mybir.dt.uint32
U8 = mybir.dt.uint8
FP8 = mybir.dt.float8_e4m3fn
FP8X4 = mybir.dt.float8_e4m3fn_x4
ACT = mybir.ActivationFunctionType
MULT = mybir.AluOpType.mult
ADD = mybir.AluOpType.add

P = 128
SEG = P + B
XV_ROW = J * SEG + SEG
XV_SLOTS = 5
BANK_TAPS = ([(0, 0), (0, 2), (1, 0)], [(1, 2), (2, 0), (2, 2)])
SPARE = 3
LOAD_AHEAD = 9
FIRST_STEP = -7


def tile_bottleneckinvolutionthreebythree_t_kernel(tc, x, w1, b1, g1, w2_bytes, w2_scale, gv, out):
    nc = tc.nc

    def inside(row):
        return 0 <= row < H

    def interior(row):
        return 0 < row < H - 1

    with ExitStack() as ctx:
        keep = ctx.enter_context(tc.tile_pool(name="keep", bufs=1))
        work = ctx.enter_context(tc.tile_pool(name="work", bufs=2))
        prods = ctx.enter_context(tc.tile_pool(name="prods", bufs=3))
        psum = ctx.enter_context(tc.psum_pool(name="psum", bufs=2))
        ctx.enter_context(tc.manual_schedule())

        x_pairs, mx_words, inv_words, x_grouped, x_quant = {}, {}, {}, {}, {}
        z_grouped, z_quant, k_banks, k_mid, prod_v, prod_g, out_rows = {}, {}, {}, {}, {}, {}, {}

        def load_pair(row):
            pair = work.tile([P, 2, C], BF16, name="x_pair", bufs=4)
            for b in range(B):
                nc.sync.dma_start(out=pair[b:P:B, :, :], in_=x[b, row:row + 2].rearrange("i w c -> w i c"))
            x_pairs[row] = pair

        load_pair(0)
        w1_raw = prods.tile([P, 2, 4, R], BF16, name="w1_raw", tag="pg", align_bytes=64)
        for half in range(2):
            nc.sync.dma_start(out=w1_raw[:, half],
                              in_=w1[512 * half:512 * (half + 1), :].rearrange("(p j) r -> p j r", j=4))
        w2_rows = w2_bytes.rearrange("(p t) n -> p t n", t=4)
        w2_raw = []
        for half in range(2):
            raw_bytes = keep.tile([P, 2, O], U8, name="w2_raw%d" % half)
            nc.sync.dma_start(out=raw_bytes[:], in_=w2_rows[:, 2 * half:2 * half + 2, :])
            w2_raw.append(raw_bytes)
        w2_sc = keep.tile([P, 4], F32, name="w2_sc")
        nc.sync.dma_start(out=w2_sc[:], in_=w2_scale.rearrange("(p t) o -> p (t o)", t=4))
        b1_raw = keep.tile([P, 4], BF16, name="b1_raw")
        nc.sync.dma_start(out=b1_raw[:], in_=b1.rearrange("(p t) -> p t", t=4))
        g1_raw = keep.tile([P, 4], BF16, name="g1_raw")
        nc.sync.dma_start(out=g1_raw[:], in_=g1.rearrange("(p t) -> p t", t=4))
        gv_raw = keep.tile([P, J], BF16, name="gv_raw")
        nc.sync.dma_start(out=gv_raw[:], in_=gv.rearrange("(p j) -> p j", j=J))

        ident = keep.tile([P, P], F32, name="ident")
        make_identity(nc, ident[:])
        zeros = keep.tile([P, P], BF16, name="zeros")
        nc.gpsimd.memset(zeros[:], 0.0)
        xv = keep.tile([P, XV_SLOTS, XV_ROW], F32, name="xv")
        for slot in range(XV_SLOTS):
            nc.gpsimd.memset(xv[:, slot].rearrange("p (j c) -> p j c", c=SEG)[:, :, 0:B], 0.0)

        w1_grouped = prods.tile([P, 2, R, 4], BF16, name="w1_grouped", tag="pg", align_bytes=64)
        for half in range(2):
            nc.vector.tensor_copy(out=w1_grouped[:, half].rearrange("p (t m) j -> p t m j", t=4),
                                  in_=w1_raw[:, half].rearrange("p j (m t) -> p t m j", t=4))
        w1_codes = keep.tile([P, 2, R], U32, name="w1_codes", align_bytes=64)
        w1_scales = keep.tile([P, 2, R], U8, name="w1_scales", align_bytes=64)
        nc.vector.quantize_mx(out=w1_codes[:].rearrange("p g r -> p (g r)").bitcast(FP8X4),
                              scales=w1_scales[:].rearrange("p g r -> p (g r)"),
                              in_=w1_grouped[:].rearrange("p g r j -> p (g r j)"))
        b1_col = keep.tile([P, 4], F32, name="b1_col")
        g1_col = keep.tile([P, 4], F32, name="g1_col")
        gv_col = keep.tile([P, J], F32, name="gv_col")
        nc.vector.tensor_copy(out=b1_col[:], in_=b1_raw[:])
        nc.vector.tensor_copy(out=g1_col[:], in_=g1_raw[:])
        nc.vector.tensor_copy(out=gv_col[:], in_=gv_raw[:])

        w2_codes = keep.tile([P, O], U32, name="w2_codes", align_bytes=64)
        w2_scales = keep.tile([P, O], U8, name="w2_scales", align_bytes=64)

        def prepare_w2():
            planes = prods.tile([P, 4, O], BF16, name="w2_planes", tag="pg", align_bytes=64)
            for t in range(4):
                nc.vector.tensor_scalar(out=planes[:, t, :], in0=w2_raw[t // 2][:, t % 2, :].bitcast(FP8),
                                        scalar1=w2_sc[:, t:t + 1], scalar2=None, op0=MULT)
            grouped = prods.tile([P, O, 4], BF16, name="w2_grouped", tag="pv", align_bytes=64)
            nc.vector.tensor_copy(out=grouped[:].rearrange("p (c i) t -> p c t i", i=4),
                                  in_=planes[:].rearrange("p t (c i) -> p c t i", i=4))
            for lo, hi in ((0, 1024), (1024, O)):
                nc.vector.quantize_mx(out=w2_codes[:, lo:hi].bitcast(FP8X4), scales=w2_scales[:, lo:hi],
                                      in_=grouped[:, lo:hi, :].rearrange("p c t -> p (c t)"))

        def row_words(row):
            return x_pairs[row - row % 2][:, row % 2, :].bitcast(F32)

        def arrange_mx(row):
            words = work.tile([P, 512], F32, name="mx_words")
            nc.scalar.copy(out=words[:].rearrange("p (g u q i) -> p g q u i", g=2, u=2, i=4),
                           in_=row_words(row).rearrange("p (g q i u) -> p g q u i", g=2, i=4, u=2))
            mx_words[row] = words

        def arrange_inv(row):
            words = work.tile([P, 512], F32, name="inv_words")
            nc.scalar.copy(out=words[:].rearrange("p (u q i) -> p q u i", u=4, i=4),
                           in_=row_words(row).rearrange("p (q i u) -> p q u i", i=4, u=4))
            inv_words[row] = words

        def turn(words):
            bank = psum.tile([P, 4, P], F32, name="misc")
            for n in range(4):
                nc.tensor.transpose(bank[:, n, :], words[:, P * n:P * (n + 1)], ident[:])
            return bank

        def empty_mx(row, bank):
            if row % 2 == 0:
                x_grouped[row] = work.tile([P, 2, 2, P * 4], BF16, name="x_grouped", align_bytes=64)
            grouped = x_grouped[row - row % 2]
            nc.scalar.copy(out=grouped[:, :, row % 2, :].bitcast(F32).rearrange("p g (q u) -> p g q u", u=2),
                           in_=bank[:].rearrange("p (g u) q -> p g q u", u=2))

        def empty_inv(row, bank):
            halves = bank[:].bitcast(BF16).rearrange("p u (q e) -> p u q e", e=2)
            for j in range(J):
                lo = j * SEG + B
                nc.scalar.activation(out=xv[:, row % XV_SLOTS, lo:lo + P], in_=halves[:, j // 2, :, j % 2],
                                     func=ACT.Copy, scale=gv_col[:, j:j + 1])

        def quantize_x(row):
            codes = work.tile([P, 2, 2, P], U32, name="x_codes", align_bytes=64)
            scales = work.tile([P, 2, 2, P], U8, name="x_scales", align_bytes=64)
            nc.vector.quantize_mx(out=codes[:].rearrange("p g h q -> p (g h q)").bitcast(FP8X4),
                                  scales=scales[:].rearrange("p g h q -> p (g h q)"),
                                  in_=x_grouped[row][:].rearrange("p g h c -> p (g h c)"))
            x_quant[row] = (codes, scales)

        def quantize_z(row):
            codes = work.tile([P, 2, P], U32, name="z_codes", align_bytes=64)
            scales = work.tile([P, 2, P], U8, name="z_scales", align_bytes=64)
            nc.vector.quantize_mx(out=codes[:].rearrange("p h q -> p (h q)").bitcast(FP8X4),
                                  scales=scales[:].rearrange("p h q -> p (h q)"),
                                  in_=z_grouped[row][:].rearrange("p h q t -> p (h q t)"))
            z_quant[row] = (codes, scales)

        def hidden_matmuls(row):
            codes, scales = x_quant[row - row % 2]
            bank = psum.tile([P, 4, P], F32, name="misc")
            for t in range(4):
                cols = slice(P * t, P * (t + 1))
                for half in range(2):
                    nc.tensor.matmul_mx(out=bank[:, t, :],
                                        lhsT=w1_codes[:, half, cols].bitcast(FP8X4), lhsT_scale=w1_scales[:, half, cols],
                                        rhs=codes[:, half, row % 2, :].bitcast(FP8X4), rhs_scale=scales[:, half, row % 2, :],
                                        start=(half == 0), stop=(half == 1))
            return bank

        def activate(row, bank):
            gated = work.tile([P, 4, P], F32, name="gated")
            for t in range(4):
                nc.scalar.activation(out=gated[:, t, :], in_=bank[:, t, :], func=ACT.Silu, bias=b1_col[:, t:t + 1])
            if row % 2 == 0:
                z_grouped[row] = work.tile([P, 2, P, 4], BF16, name="z_grouped", align_bytes=64)
            grouped = z_grouped[row - row % 2][:, row % 2]
            if row < 4:
                nc.vector.tensor_tensor(out=grouped, in0=gated[:].rearrange("p t q -> p q t"),
                                        in1=g1_col[:].unsqueeze(1).to_broadcast([P, P, 4]), op=MULT)
                return
            planes = work.tile([P, 4, P], BF16, name="z_planes")
            for t in range(4):
                nc.scalar.activation(out=planes[:, t, :], in_=gated[:, t, :], func=ACT.Copy, scale=g1_col[:, t:t + 1])
            nc.scalar.copy(out=grouped.rearrange("p (c i) t -> p c t i", i=4),
                           in_=planes[:].rearrange("p t (c i) -> p c t i", i=4))

        def tap_matmul(row, tap, dest):
            codes, scales = z_quant[row - row % 2]
            n = 3 * tap[0] + tap[1]
            cols = slice(G * n, G * (n + 1))
            nc.tensor.matmul_mx(out=dest, lhsT=w2_codes[:, cols].bitcast(FP8X4), lhsT_scale=w2_scales[:, cols],
                                rhs=codes[:, row % 2, :].bitcast(FP8X4), rhs_scale=scales[:, row % 2, :],
                                start=True, stop=True)

        def mid_rows(row):
            return [di for di in range(3) if inside(row + di - 1)]

        def mid_matmuls(row):
            mid_bank = psum.tile([P, 4, P], F32, name="misc")
            by_scalar = [di for di in mid_rows(row) if di == 0 or (di == 1 and row % 2 == 0)]
            for di in by_scalar:
                tap_matmul(row, (di, 1), mid_bank[:, di, :])
            return mid_bank, by_scalar

        def side_matmuls(row):
            banks = []
            for n, taps in enumerate(BANK_TAPS):
                bank = psum.tile([P, 4, P], F32, name="k_bank%d" % n)
                for s, tap in enumerate(taps):
                    if inside(row + tap[0] - 1):
                        tap_matmul(row, tap, bank[:, s, :])
                if n == 0 and row % 2 == 1:
                    tap_matmul(row, (1, 1), bank[:, SPARE, :])
                if n == 1 and inside(row + 1):
                    tap_matmul(row, (2, 1), bank[:, SPARE, :])
                banks.append(bank)
            k_banks[row] = banks

        def empty_mid(row, mid_bank, by_scalar):
            mid = work.tile([P, 2, P], F32, name="k_mid", bufs=3)
            sel = slice(by_scalar[0], by_scalar[-1] + 1)
            nc.scalar.copy(out=mid[:, sel, :], in_=mid_bank[:, sel, :])
            k_mid[row] = mid

        def shifted(row, dj):
            lo = B * dj
            return xv[:, row % XV_SLOTS, lo:lo + J * SEG].rearrange("p (j c) -> p j c", c=SEG)[:, :, 0:P]

        def side_products(row):
            prod = prods.tile([P, 6, J, P], F32, name="prod_v", tag="pv", align_bytes=64)
            for n, taps in enumerate(BANK_TAPS):
                for s, (di, dj) in enumerate(taps):
                    if inside(row + di - 1):
                        nc.vector.tensor_tensor(out=prod[:, 3 * n + s],
                                                in0=k_banks[row][n][:, s, :].unsqueeze(1).to_broadcast([P, J, P]),
                                                in1=shifted(row + di - 1, dj), op=MULT)
            if inside(row + 1):
                nc.vector.tensor_tensor(out=prod_g[row][:, 2],
                                        in0=k_banks[row][1][:, SPARE, :].unsqueeze(1).to_broadcast([P, J, P]),
                                        in1=shifted(row + 1, 1), op=MULT)
            prod_v[row] = prod

        def mid_products(row):
            prod = prods.tile([P, 3, J, P], F32, name="prod_g", tag="pg", align_bytes=64)
            runs = []
            for di in mid_rows(row):
                if di == 2:
                    continue
                if runs and (row + di - 1) % XV_SLOTS != 0:
                    runs[-1].append(di)
                else:
                    runs.append([di])
            for run in runs:
                lo, n = run[0], len(run)
                slot = (row + lo - 1) % XV_SLOTS
                window = xv[:, slot:slot + n, B:B + J * SEG].rearrange("p d (j c) -> p d j c", c=SEG)[:, :, :, 0:P]
                nc.gpsimd.tensor_tensor(out=prod[:, lo:lo + n],
                                        in0=k_mid[row][:, lo:lo + n, :].unsqueeze(2).to_broadcast([P, n, J, P]),
                                        in1=window, op=MULT)
            prod_g[row] = prod

        def side_terms(row):
            return [prod_v[row][:, 3 * n + s] for n, taps in enumerate(BANK_TAPS)
                    for s, tap in enumerate(taps) if inside(row + tap[0] - 1)]

        def add_first_pair(row):
            first, second = side_terms(row)[0:2]
            nc.gpsimd.tensor_tensor(out=first, in0=first, in1=second, op=ADD)

        def sum_taps(row, half):
            sides = side_terms(row)
            mids = [prod_g[row][:, di] for di in mid_rows(row)]
            terms = sides[2:] + mids + sides[0:1] if interior(row) else sides + mids
            bank = psum.tile([P, 4, P], F32, name="out_bank")
            for jj in range(4):
                opened = jj > 0
                if opened:
                    nc.tensor.matmul(bank[:, jj, :], lhsT=zeros[:], rhs=zeros[:], start=True, stop=False)
                for n, term in enumerate(terms):
                    nc.tensor.matmul(bank[:, jj, :], lhsT=term[:, 4 * half + jj, :], rhs=ident[:], is_transpose=True,
                                     start=(n == 0 and not opened), stop=(n == len(terms) - 1))
            if half == 0:
                out_rows[row] = work.tile([P, G, J], F32, name="out_row", bufs=3)
            nc.scalar.copy(out=out_rows[row][:, :, 4 * half:4 * half + 4], in_=bank[:].rearrange("p j g -> p g j"))

        def store_row(row):
            flat = out_rows[row][:].rearrange("p g j -> p (g j)")
            for b in range(B):
                nc.sync.dma_start(out=out[b, row], in_=flat[b:P:B, :])

        for m in range(FIRST_STEP, H):
            if m % 2 == 1 and inside(m + LOAD_AHEAD):
                load_pair(m + LOAD_AHEAD)
            if m % 2 == 0:
                if inside(m + 4):
                    quantize_x(m + 4)
                if m == -4:
                    prepare_w2()
                if inside(m + 2):
                    quantize_z(m + 2)
                if inside(m + 1):
                    nc.vector.tensor_copy(out=k_mid[m + 1][:, 1, :], in_=k_banks[m + 1][0][:, SPARE, :])
            if inside(m + 1):
                mid_products(m + 1)
                side_products(m + 1)
                if interior(m + 1):
                    add_first_pair(m + 1)
            if inside(m + 6):
                mx_bank = turn(mx_words[m + 6])
            if inside(m + 3):
                inv_bank = turn(inv_words[m + 3])
            if inside(m + 6):
                empty_mx(m + 6, mx_bank)
            if inside(m + 3):
                empty_inv(m + 3, inv_bank)
            if inside(m + 7):
                arrange_mx(m + 7)
            if inside(m + 4):
                arrange_inv(m + 4)
            if inside(m):
                sum_taps(m, 0)
            if inside(m + 4):
                hidden_bank = hidden_matmuls(m + 4)
            if inside(m + 2):
                mid_bank, by_scalar = mid_matmuls(m + 2)
                side_matmuls(m + 2)
            if inside(m + 4):
                activate(m + 4, hidden_bank)
            if inside(m + 2):
                empty_mid(m + 2, mid_bank, by_scalar)
            if inside(m):
                sum_taps(m, 1)
                store_row(m)
